import numpy as np
import ml_dtypes


def mxq(x, axis, fmt="e4m3"):
    dtype, down = {"e4m3": (ml_dtypes.float8_e4m3fn, 7), "e5m2": (ml_dtypes.float8_e5m2, 14)}[fmt]
    v = np.moveaxis(np.asarray(x, np.float32).astype(ml_dtypes.bfloat16).astype(np.float64), axis, -1)
    blocks = v.reshape(v.shape[:-1] + (-1, 32))
    amax = np.abs(blocks).max(-1, keepdims=True)
    byte = np.maximum(np.where(amax > 0, np.frexp(amax)[1] - 1 + 127, 0) - down, 1)
    scale = np.exp2(byte - 127.0)
    codes = (blocks / scale).astype(np.float32).astype(dtype).astype(np.float64)
    return np.moveaxis((codes * scale).reshape(v.shape), -1, axis)


WIDE = False


def mx_kscale(k):
    if not WIDE:
        return np.ones(k)
    levels = np.array([10, -10, 5, -5, 0])
    if k % 512:
        return np.exp2(np.random.permutation(np.resize(levels, k // 32))).repeat(32)
    a = np.empty((k // 512, 16))
    for p in range(k // 512):
        a[p, :8] = np.random.permutation(np.resize(levels, 8))
        for g in range(8):
            far = levels[np.abs(levels - a[p, g]) >= 10]
            a[p, g + 8] = far[np.random.randint(len(far))]
    return np.exp2(a.ravel()).repeat(32)


def f64(x):
    return np.asarray(x).astype(np.float64)


def striped8(idx):
    return np.concatenate([v.reshape(-1, 16).T for v in idx]).astype(np.uint16)


def unstriped8(offs):
    return np.stack([offs[16 * g:16 * g + 16].T.reshape(-1) for g in range(8)]).astype(np.int64)


E2M1 = np.array([0.0, 0.5, 1.0, 1.5, 2.0, 3.0, 4.0, 6.0, -0.0, -0.5, -1.0, -1.5, -2.0, -3.0, -4.0, -6.0])


def pack_weight(w, fmt):
    k, n = w.shape
    w = f64(np.asarray(w, np.float32).astype(ml_dtypes.bfloat16)).reshape(k // 32, 32, n)
    amax = np.abs(w).max(1)
    if fmt == "e4m3":
        byte = np.frexp(amax)[1] - 1 + 127 - 7
    else:
        mant, ex = np.frexp(amax / 6.0)
        byte = np.where(mant > 0.5, ex, ex - 1) + 127
    byte = np.clip(np.where(amax > 0, byte, 1), 1, 254)
    scaled = (w * np.exp2(127.0 - byte)[:, None, :]).reshape(k, n).astype(np.float32)
    by_word = np.ascontiguousarray(scaled.reshape(k // 512, 128, 4, n).transpose(0, 1, 3, 2))
    if fmt == "e4m3":
        words = by_word.astype(ml_dtypes.float8_e4m3fn).view(np.uint8)
    else:
        c = by_word.astype(ml_dtypes.float4_e2m1fn).view(np.uint8) & 0xF
        words = (c[..., 0::2] | (c[..., 1::2] << 4)).reshape(k // 512, 128, 2 * n)
    return np.ascontiguousarray(words), np.ascontiguousarray(byte.astype(np.uint8).reshape(k // 512, 16, n))


def unpack_weight(words, scales, fmt):
    g, _, n = scales.shape
    words = np.ascontiguousarray(words).reshape(g, 128, n, -1)
    if fmt == "e4m3":
        vals = words.view(ml_dtypes.float8_e4m3fn).astype(np.float64)
    else:
        nib = np.empty((g, 128, n, 4), np.uint8)
        nib[..., 0::2] = words & 0xF
        nib[..., 1::2] = words >> 4
        vals = E2M1[nib]
    vals = vals * np.repeat(np.exp2(scales.astype(np.float64) - 127.0), 8, axis=1)[..., None]
    return vals.transpose(0, 1, 3, 2).reshape(g * 512, n)


def gelu(v):
    return 0.5 * v * (1.0 + np.tanh(np.sqrt(2.0 / np.pi) * (v + 0.044715 * v**3)))


K, L, M, T, S = 1536, 1024, 512, 1024, 512


def setup_inputs():
    n = np.random.standard_normal
    s1 = mx_kscale(K)[:, None]
    s2 = mx_kscale(L)[:, None]
    p_w4 = pack_weight(n((K, M)) / np.sqrt(K) / s1, "e2m1")
    return {
        "xT": (n((K, T)) * s1).astype(np.float32),
        "w4_words": p_w4[0],
        "w4_scales": p_w4[1],
        "c": (n((L, S)) * s2).astype(np.float32),
        "u": (n((L, M)) / np.sqrt(L) / s2).astype(np.float32),
        "wgt": np.repeat(np.random.uniform(0.5, 2.0, (8, S)), 16, axis=0).astype(np.float32),
        "b": (0.3 * n(512)).astype(np.float32),
        "offs": striped8(np.stack([np.random.permutation(T)[:S] for _ in range(8)])),
    }


def reference(xT, w4_words, w4_scales, c, u, wgt, b, offs):
    idx = unstriped8(offs)
    group = np.arange(K) % 512 // 64
    xg = f64(wgt)[np.arange(K) // 4 % 128] * f64(xT)[np.arange(K)[:, None], idx[group]]
    xT_ = mxq(xg, 0, "e4m3")
    w4_ = unpack_weight(w4_words, w4_scales, "e2m1")
    c_ = mxq(f64(c), 0, "e4m3")
    u_ = mxq(f64(u), 0, "e4m3")
    y = w4_.T @ xT_ + u_.T @ c_
    return gelu(y + f64(b)[:, None])

@@ -1,0 +1,181 @@
+from contextlib import ExitStack
+
+import concourse.mybir as mybir
+from concourse.masks import make_identity
+
+K, L, M, T, S = 1536, 1024, 512, 1024, 512
+FLOPS = 2 * M * S * (K + L)
+
+F32 = mybir.dt.float32
+BF16 = mybir.dt.bfloat16
+I32 = mybir.dt.int32
+U32 = mybir.dt.uint32
+U16 = mybir.dt.uint16
+U8 = mybir.dt.uint8
+FP8X4 = mybir.dt.float8_e4m3fn_x4
+FP4X4 = mybir.dt.float4_e2m1fn_x4
+MULT = mybir.AluOpType.mult
+GELU = mybir.ActivationFunctionType.Gelu_apprx_tanh
+
+P = 128
+KP = 512
+NX, NC = K // KP, L // KP
+NM = M // P
+H = S // 2
+
+
+def tile_list_hmix_gelu_kernel(tc, xT, w4_words, w4_scales, c, u, wgt, b, offs, out):
+    nc = tc.nc
+    with ExitStack() as ctx:
+        keep = ctx.enter_context(tc.tile_pool(name="keep", bufs=1))
+        psum = ctx.enter_context(tc.psum_pool(name="psum", bufs=1))
+
+        def held(shape, dtype, name):
+            return keep.tile(shape, dtype, name=name, tag=name, align_bytes=64)
+
+        offsets = keep.tile([P, S // 16], U16, name="offsets")
+        weight = held([P, S], F32, "weight")
+        planes = [[held([P, T], F32, "plane%d_%d" % (a, i)) for i in range(4)] for a in range(NX)]
+        picked = [held([P, 4, S], F32, "picked%d" % a) for a in range(NX)]
+        c_raw = [held([P, 4, S], F32, "c_raw%d" % a) for a in range(NC)]
+        u_raw = [held([P, 4, M], F32, "u_raw%d" % a) for a in range(NC)]
+        x_mix = [held([P, S, 4], BF16, "x_mix%d" % a) for a in range(NX)]
+        c_mix = [held([P, S, 4], BF16, "c_mix%d" % a) for a in range(NC)]
+        u_mix = [held([P, M, 4], BF16, "u_mix%d" % a) for a in range(NC)]
+        x_codes = [held([P, S], U32, "x_codes%d" % a) for a in range(NX)]
+        c_codes = [held([P, S], U32, "c_codes%d" % a) for a in range(NC)]
+        u_codes = [held([P, M], U32, "u_codes%d" % a) for a in range(NC)]
+        x_scale = [held([P, S], U8, "x_scale%d" % a) for a in range(NX)]
+        c_scale = [held([P, S], U8, "c_scale%d" % a) for a in range(NC)]
+        u_scale = [held([P, M], U8, "u_scale%d" % a) for a in range(NC)]
+        w_words = held([P, NX, 2 * M], U8, "w_words")
+        w_scale = held([P, NX, M], U8, "w_scale")
+        b_rows = held([P, P], F32, "b_rows")
+        b_cols = held([P, NM], F32, "b_cols")
+        ident = held([P, P], F32, "ident")
+        warm = held([P, 1], F32, "warm")
+        result = [held([P, S], F32, "result%d" % m) for m in range(NM)]
+        sums = [psum.tile([P, S], F32, name="sums%d" % m, tag="sums%d" % m) for m in range(NM)]
+        b_turned = psum.tile([P, P], F32, name="b_turned")
+
+        def load_plane(a, i):
+            rows = xT[KP * a : KP * (a + 1), :].rearrange("(p i) t -> p i t", i=4)
+            nc.sync.dma_start(planes[a][i][:], rows[:, i, :])
+
+        def load_raw(tiles, src, a, lo, hi):
+            rows = src[KP * a : KP * (a + 1), :].rearrange("(p i) w -> p i w", i=4)
+            nc.sync.dma_start(tiles[a][:, :, lo:hi], rows[:, :, lo:hi])
+
+        def gather(a, i):
+            for h in range(2):
+                cols = slice(h * H, (h + 1) * H)
+                nc.vector.tensor_tensor(
+                    picked[a][:, i, cols],
+                    planes[a][i][:].indirect(offsets[:, h * H // 16 : (h + 1) * H // 16]),
+                    weight[:, cols],
+                    MULT,
+                )
+
+        def mix(on_scalar, mixed, raw, lo, hi):
+            src = raw[:, :, lo:hi].rearrange("p i w -> p w i")
+            if on_scalar:
+                nc.scalar.copy(mixed[:, lo:hi, :], src)
+            else:
+                nc.vector.tensor_copy(mixed[:, lo:hi, :], src)
+
+        def quantise(codes, scale, mixed, lo, hi):
+            nc.vector.quantize_mx(
+                out=codes[:, lo:hi].bitcast(FP8X4),
+                scales=scale[:, lo:hi],
+                in_=mixed[:, lo:hi, :].rearrange("p w i -> p (w i)"),
+            )
+
+        def times_w4(a, start):
+            for m in range(NM):
+                nc.tensor.matmul_mx(
+                    out=sums[m][:],
+                    lhsT=w_words[:, a, 2 * P * m : 2 * P * (m + 1)].bitcast(FP4X4),
+                    lhsT_scale=w_scale[:, a, P * m : P * (m + 1)],
+                    rhs=x_codes[a][:].bitcast(FP8X4),
+                    rhs_scale=x_scale[a][:],
+                    start=start,
+                    stop=False,
+                )
+
+        def times_u(a, m, stop):
+            cols = slice(P * m, P * (m + 1))
+            nc.tensor.matmul_mx(
+                out=sums[m][:],
+                lhsT=u_codes[a][:, cols].bitcast(FP8X4),
+                lhsT_scale=u_scale[a][:, cols],
+                rhs=c_codes[a][:].bitcast(FP8X4),
+                rhs_scale=c_scale[a][:],
+                start=False,
+                stop=stop,
+            )
+
+        nc.gpsimd.memset(w_scale[:].rearrange("p a n -> p (a n)").bitcast(I32), 0)
+        nc.gpsimd.memset(b_rows[:], 0.0)
+        nc.gpsimd.memset(warm[:], 0.0)
+        make_identity(nc, ident[:])
+        nc.scalar.activation(warm[:], warm[:], GELU)
+
+        nc.sync.dma_start(offsets[:], offs)
+        nc.sync.dma_start(weight[:, 0:H], wgt[:, 0:H])
+        load_plane(0, 0)
+        nc.sync.dma_start(weight[:, H:S], wgt[:, H:S])
+        for i in range(1, 4):
+            load_plane(0, i)
+        for q in range(4):
+            nc.scalar.dma_start(
+                w_scale[32 * q : 32 * q + 4, :, :].bitcast(I32),
+                w4_scales[:, 4 * q : 4 * q + 4, :].rearrange("a r n -> r a n").bitcast(I32),
+            )
+        nc.scalar.dma_start(b_rows[0:NM, :], b.rearrange("(m p) -> m p", p=P))
+        load_raw(c_raw, c, 0, 0, S)
+        for i in range(4):
+            load_plane(1, i)
+        nc.sync.dma_start(w_words[:], w4_words.rearrange("a p n -> p a n"))
+        for i in range(4):
+            load_plane(2, i)
+        load_raw(c_raw, c, 1, 0, S)
+        load_raw(u_raw, u, 0, 0, M)
+        load_raw(u_raw, u, 1, 0, H)
+        load_raw(u_raw, u, 1, H, M)
+
+        nc.tensor.transpose(b_turned[:], b_rows[:], ident[:])
+        nc.scalar.copy(b_cols[:], b_turned[:, 0:NM])
+
+        for i in range(4):
+            gather(0, i)
+        mix(True, x_mix[0], picked[0], 0, S)
+        mix(True, c_mix[0], c_raw[0], 0, S)
+        for i in range(4):
+            gather(1, i)
+        mix(True, x_mix[1], picked[1], 0, S)
+        for i in range(4):
+            gather(2, i)
+        mix(True, x_mix[2], picked[2], H, S)
+        mix(True, u_mix[0], u_raw[0], 0, H)
+        mix(True, u_mix[0], u_raw[0], H, M)
+        mix(True, u_mix[1], u_raw[1], 0, H)
+        quantise(x_codes[0], x_scale[0], x_mix[0], 0, S)
+        times_w4(0, True)
+        quantise(c_codes[0], c_scale[0], c_mix[0], 0, S)
+        quantise(x_codes[1], x_scale[1], x_mix[1], 0, S)
+        times_w4(1, False)
+        mix(False, x_mix[2], picked[2], 0, H)
+        mix(False, c_mix[1], c_raw[1], 0, S)
+        quantise(c_codes[1], c_scale[1], c_mix[1], 0, S)
+        quantise(x_codes[2], x_scale[2], x_mix[2], 0, S)
+        times_w4(2, False)
+        mix(False, u_mix[1], u_raw[1], H, M)
+        quantise(u_codes[0], u_scale[0], u_mix[0], 0, M)
+        for m in range(NM):
+            times_u(0, m, False)
+        for h in range(2):
+            quantise(u_codes[1], u_scale[1], u_mix[1], h * H, (h + 1) * H)
+            for m in (2 * h, 2 * h + 1):
+                times_u(1, m, True)
+                nc.scalar.activation(result[m][:], sums[m][:], GELU, bias=b_cols[:, m : m + 1])
+                nc.sync.dma_start(out[P * m : P * (m + 1), :], result[m][:])

@@ -40,11 +40,11 @@ def tile_list_hmix_gelu_kernel(tc, xT, w4_words, w4_scales, c, u, wgt, b, offs, 
         c_raw = [held([P, 4, S], F32, "c_raw%d" % a) for a in range(NC)]
         u_raw = [held([P, 4, M], F32, "u_raw%d" % a) for a in range(NC)]
         x_mix = [held([P, S, 4], BF16, "x_mix%d" % a) for a in range(NX)]
-        c_mix = [held([P, S, 4], BF16, "c_mix%d" % a) for a in range(NC)]
-        u_mix = [held([P, M, 4], BF16, "u_mix%d" % a) for a in range(NC)]
-        x_codes = [held([P, S], U32, "x_codes%d" % a) for a in range(NX)]
-        c_codes = [held([P, S], U32, "c_codes%d" % a) for a in range(NC)]
-        u_codes = [held([P, M], U32, "u_codes%d" % a) for a in range(NC)]
+        c_mix = [None, held([P, S, 4], BF16, "c_mix1")]
+        u_mix = [held([P, M, 4], BF16, "u_mix0"), None]
+        x_codes = [None] * NX
+        c_codes = [None] * NC
+        u_codes = [None] * NC
         x_scale = [held([P, S], U8, "x_scale%d" % a) for a in range(NX)]
         c_scale = [held([P, S], U8, "c_scale%d" % a) for a in range(NC)]
         u_scale = [held([P, M], U8, "u_scale%d" % a) for a in range(NC)]
@@ -57,6 +57,9 @@ def tile_list_hmix_gelu_kernel(tc, xT, w4_words, w4_scales, c, u, wgt, b, offs, 
         result = [held([P, S], F32, "result%d" % m) for m in range(NM)]
         sums = [psum.tile([P, S], F32, name="sums%d" % m, tag="sums%d" % m) for m in range(NM)]
         b_turned = psum.tile([P, P], F32, name="b_turned")
+
+        def instead(tag, shape, dtype, name):
+            return keep.tile(shape, dtype, name=name, tag=tag, align_bytes=64)
 
         def load_plane(a, i):
             rows = xT[KP * a : KP * (a + 1), :].rearrange("(p i) t -> p i t", i=4)
@@ -132,14 +135,15 @@ def tile_list_hmix_gelu_kernel(tc, xT, w4_words, w4_scales, c, u, wgt, b, offs, 
                 w4_scales[:, 4 * q : 4 * q + 4, :].rearrange("a r n -> r a n").bitcast(I32),
             )
         nc.scalar.dma_start(b_rows[0:NM, :], b.rearrange("(m p) -> m p", p=P))
-        load_raw(c_raw, c, 0, 0, S)
         for i in range(4):
             load_plane(1, i)
+        load_raw(u_raw, u, 0, 0, M)
         nc.sync.dma_start(w_words[:], w4_words.rearrange("a p n -> p a n"))
-        for i in range(4):
+        for i in range(3):
             load_plane(2, i)
         load_raw(c_raw, c, 1, 0, S)
-        load_raw(u_raw, u, 0, 0, M)
+        load_plane(2, 3)
+        load_raw(c_raw, c, 0, 0, S)
         load_raw(u_raw, u, 1, 0, H)
         load_raw(u_raw, u, 1, H, M)
 
@@ -149,31 +153,41 @@ def tile_list_hmix_gelu_kernel(tc, xT, w4_words, w4_scales, c, u, wgt, b, offs, 
         for i in range(4):
             gather(0, i)
         mix(True, x_mix[0], picked[0], 0, S)
-        mix(True, c_mix[0], c_raw[0], 0, S)
         for i in range(4):
             gather(1, i)
-        mix(True, x_mix[1], picked[1], 0, S)
-        for i in range(4):
-            gather(2, i)
-        mix(True, x_mix[2], picked[2], H, S)
         mix(True, u_mix[0], u_raw[0], 0, H)
         mix(True, u_mix[0], u_raw[0], H, M)
-        mix(True, u_mix[1], u_raw[1], 0, H)
+        mix(True, x_mix[1], picked[1], 0, S)
+        x_codes[0] = instead("plane1_3", [P, S], U32, "x_codes0")
         quantise(x_codes[0], x_scale[0], x_mix[0], 0, S)
         times_w4(0, True)
-        quantise(c_codes[0], c_scale[0], c_mix[0], 0, S)
+        for i in range(3):
+            gather(2, i)
+        mix(True, c_mix[1], c_raw[1], 0, S)
+        u_codes[0] = instead("plane2_2", [P, M], U32, "u_codes0")
+        x_codes[1] = instead("plane2_1", [P, S], U32, "x_codes1")
+        quantise(u_codes[0], u_scale[0], u_mix[0], 0, M)
         quantise(x_codes[1], x_scale[1], x_mix[1], 0, S)
         times_w4(1, False)
-        mix(False, x_mix[2], picked[2], 0, H)
-        mix(False, c_mix[1], c_raw[1], 0, S)
+        gather(2, 3)
+        mix(True, x_mix[2], picked[2], 0, H)
+        mix(False, x_mix[2], picked[2], H, S)
+        c_codes[1] = instead("plane2_3", [P, S], U32, "c_codes1")
+        c_mix[0] = instead("plane2_0", [P, S, 4], BF16, "c_mix0")
+        x_codes[2] = held([P, S], U32, "x_codes2")
+        c_codes[0] = held([P, S], U32, "c_codes0")
+        u_codes[1] = held([P, M], U32, "u_codes1")
         quantise(c_codes[1], c_scale[1], c_mix[1], 0, S)
+        mix(False, c_mix[0], c_raw[0], 0, H)
+        mix(True, c_mix[0], c_raw[0], H, S)
         quantise(x_codes[2], x_scale[2], x_mix[2], 0, S)
+        quantise(c_codes[0], c_scale[0], c_mix[0], 0, S)
+        u_mix[1] = instead("x_mix2", [P, M, 4], BF16, "u_mix1")
         times_w4(2, False)
-        mix(False, u_mix[1], u_raw[1], H, M)
-        quantise(u_codes[0], u_scale[0], u_mix[0], 0, M)
         for m in range(NM):
             times_u(0, m, False)
         for h in range(2):
+            mix(False, u_mix[1], u_raw[1], h * H, (h + 1) * H)
             quantise(u_codes[1], u_scale[1], u_mix[1], h * H, (h + 1) * H)
             for m in (2 * h, 2 * h + 1):
                 times_u(1, m, True)

@@ -22,6 +22,7 @@ KP = 512
 NX, NC = K // KP, L // KP
 NM = M // P
 H = S // 2
+LATE = M - P
 
 
 def tile_list_hmix_gelu_kernel(tc, xT, w4_words, w4_scales, c, u, wgt, b, offs, out):
@@ -40,11 +41,11 @@ def tile_list_hmix_gelu_kernel(tc, xT, w4_words, w4_scales, c, u, wgt, b, offs, 
         c_raw = [held([P, 4, S], F32, "c_raw%d" % a) for a in range(NC)]
         u_raw = [held([P, 4, M], F32, "u_raw%d" % a) for a in range(NC)]
         x_mix = [held([P, S, 4], BF16, "x_mix%d" % a) for a in range(NX)]
-        c_mix = [None, held([P, S, 4], BF16, "c_mix1")]
-        u_mix = [held([P, M, 4], BF16, "u_mix0"), None]
+        c_mix = [held([P, S, 4], BF16, "c_mix%d" % a) for a in range(NC)]
+        u_mix = [held([P, M, 4], BF16, "u_mix%d" % a) for a in range(NC)]
         x_codes = [None] * NX
         c_codes = [None] * NC
-        u_codes = [None] * NC
+        u_codes = [held([P, M], U32, "u_codes%d" % a) for a in range(NC)]
         x_scale = [held([P, S], U8, "x_scale%d" % a) for a in range(NX)]
         c_scale = [held([P, S], U8, "c_scale%d" % a) for a in range(NC)]
         u_scale = [held([P, M], U8, "u_scale%d" % a) for a in range(NC)]
@@ -65,6 +66,12 @@ def tile_list_hmix_gelu_kernel(tc, xT, w4_words, w4_scales, c, u, wgt, b, offs, 
             rows = xT[KP * a : KP * (a + 1), :].rearrange("(p i) t -> p i t", i=4)
             nc.sync.dma_start(planes[a][i][:], rows[:, i, :])
 
+        def load_w_scale(q):
+            nc.sync.dma_start(
+                w_scale[32 * q : 32 * q + 4, :, :].bitcast(I32),
+                w4_scales[:, 4 * q : 4 * q + 4, :].rearrange("a r n -> r a n").bitcast(I32),
+            )
+
         def load_raw(tiles, src, a, lo, hi):
             rows = src[KP * a : KP * (a + 1), :].rearrange("(p i) w -> p i w", i=4)
             nc.sync.dma_start(tiles[a][:, :, lo:hi], rows[:, :, lo:hi])
@@ -80,11 +87,12 @@ def tile_list_hmix_gelu_kernel(tc, xT, w4_words, w4_scales, c, u, wgt, b, offs, 
                 )
 
         def mix(on_scalar, mixed, raw, lo, hi):
-            src = raw[:, :, lo:hi].rearrange("p i w -> p w i")
+            src = raw[:, :, lo:hi].rearrange("p i (g w) -> p g i w", w=4)
+            dst = mixed[:, lo:hi, :].rearrange("p (g w) i -> p g i w", w=4)
             if on_scalar:
-                nc.scalar.copy(mixed[:, lo:hi, :], src)
+                nc.scalar.copy(dst, src)
             else:
-                nc.vector.tensor_copy(mixed[:, lo:hi, :], src)
+                nc.vector.tensor_copy(dst, src)
 
         def quantise(codes, scale, mixed, lo, hi):
             nc.vector.quantize_mx(
@@ -117,6 +125,13 @@ def tile_list_hmix_gelu_kernel(tc, xT, w4_words, w4_scales, c, u, wgt, b, offs, 
                 stop=stop,
             )
 
+        def finish(m, pieces):
+            width = S // pieces
+            for j in range(pieces):
+                cols = slice(width * j, width * (j + 1))
+                nc.scalar.activation(result[m][:, cols], sums[m][:, cols], GELU, bias=b_cols[:, m : m + 1])
+                nc.sync.dma_start(out[P * m : P * (m + 1), cols], result[m][:, cols])
+
         nc.gpsimd.memset(w_scale[:].rearrange("p a n -> p (a n)").bitcast(I32), 0)
         nc.gpsimd.memset(b_rows[:], 0.0)
         nc.gpsimd.memset(warm[:], 0.0)
@@ -129,67 +144,66 @@ def tile_list_hmix_gelu_kernel(tc, xT, w4_words, w4_scales, c, u, wgt, b, offs, 
         nc.sync.dma_start(weight[:, H:S], wgt[:, H:S])
         for i in range(1, 4):
             load_plane(0, i)
-        for q in range(4):
-            nc.scalar.dma_start(
-                w_scale[32 * q : 32 * q + 4, :, :].bitcast(I32),
-                w4_scales[:, 4 * q : 4 * q + 4, :].rearrange("a r n -> r a n").bitcast(I32),
-            )
-        nc.scalar.dma_start(b_rows[0:NM, :], b.rearrange("(m p) -> m p", p=P))
-        for i in range(4):
+        for i in range(3):
             load_plane(1, i)
-        load_raw(u_raw, u, 0, 0, M)
-        nc.sync.dma_start(w_words[:], w4_words.rearrange("a p n -> p a n"))
+            load_w_scale(i)
+        load_raw(c_raw, c, 0, 0, S)
+        load_w_scale(3)
+        load_plane(1, 3)
+        nc.sync.dma_start(b_rows[0:NM, :], b.rearrange("(m p) -> m p", p=P))
         for i in range(3):
             load_plane(2, i)
         load_raw(c_raw, c, 1, 0, S)
         load_plane(2, 3)
-        load_raw(c_raw, c, 0, 0, S)
+        nc.sync.dma_start(w_words[:], w4_words.rearrange("a p n -> p a n"))
+        load_raw(u_raw, u, 0, 0, M)
         load_raw(u_raw, u, 1, 0, H)
         load_raw(u_raw, u, 1, H, M)
-
-        nc.tensor.transpose(b_turned[:], b_rows[:], ident[:])
-        nc.scalar.copy(b_cols[:], b_turned[:, 0:NM])
 
         for i in range(4):
             gather(0, i)
         mix(True, x_mix[0], picked[0], 0, S)
-        for i in range(4):
+        for i in range(3):
             gather(1, i)
-        mix(True, u_mix[0], u_raw[0], 0, H)
-        mix(True, u_mix[0], u_raw[0], H, M)
-        mix(True, x_mix[1], picked[1], 0, S)
-        x_codes[0] = instead("plane1_3", [P, S], U32, "x_codes0")
+        mix(True, c_mix[0], c_raw[0], 0, S)
+        x_codes[0] = instead("plane1_2", [P, S], U32, "x_codes0")
         quantise(x_codes[0], x_scale[0], x_mix[0], 0, S)
-        times_w4(0, True)
+        gather(1, 3)
+        mix(True, x_mix[1], picked[1], 0, S)
         for i in range(3):
             gather(2, i)
-        mix(True, c_mix[1], c_raw[1], 0, S)
-        u_codes[0] = instead("plane2_2", [P, M], U32, "u_codes0")
-        x_codes[1] = instead("plane2_1", [P, S], U32, "x_codes1")
-        quantise(u_codes[0], u_scale[0], u_mix[0], 0, M)
+        x_codes[1] = instead("plane2_2", [P, S], U32, "x_codes1")
         quantise(x_codes[1], x_scale[1], x_mix[1], 0, S)
-        times_w4(1, False)
+        mix(True, c_mix[1], c_raw[1], 0, S)
+        nc.tensor.transpose(b_turned[:], b_rows[:], ident[:])
+        nc.scalar.copy(b_cols[:], b_turned[:, 0:NM])
         gather(2, 3)
-        mix(True, x_mix[2], picked[2], 0, H)
-        mix(False, x_mix[2], picked[2], H, S)
-        c_codes[1] = instead("plane2_3", [P, S], U32, "c_codes1")
-        c_mix[0] = instead("plane2_0", [P, S, 4], BF16, "c_mix0")
-        x_codes[2] = held([P, S], U32, "x_codes2")
-        c_codes[0] = held([P, S], U32, "c_codes0")
-        u_codes[1] = held([P, M], U32, "u_codes1")
-        quantise(c_codes[1], c_scale[1], c_mix[1], 0, S)
-        mix(False, c_mix[0], c_raw[0], 0, H)
-        mix(True, c_mix[0], c_raw[0], H, S)
-        quantise(x_codes[2], x_scale[2], x_mix[2], 0, S)
+        mix(False, x_mix[2], picked[2], 0, H)
+        mix(True, x_mix[2], picked[2], H, S)
+        c_codes[0] = instead("plane2_3", [P, S], U32, "c_codes0")
+        c_codes[1] = held([P, S], U32, "c_codes1")
         quantise(c_codes[0], c_scale[0], c_mix[0], 0, S)
-        u_mix[1] = instead("x_mix2", [P, M, 4], BF16, "u_mix1")
+        quantise(c_codes[1], c_scale[1], c_mix[1], 0, S)
+        times_w4(0, True)
+        times_w4(1, False)
+        x_codes[2] = held([P, S], U32, "x_codes2")
+        quantise(x_codes[2], x_scale[2], x_mix[2], 0, S)
         times_w4(2, False)
-        for m in range(NM):
+        mix(True, u_mix[0], u_raw[0], 0, H)
+        mix(True, u_mix[0], u_raw[0], H, M)
+        mix(False, u_mix[1], u_raw[1], 0, H)
+        quantise(u_codes[0], u_scale[0], u_mix[0], 0, H)
+        quantise(u_codes[1], u_scale[1], u_mix[1], 0, H)
+        mix(True, u_mix[1], u_raw[1], H, LATE)
+        mix(False, u_mix[1], u_raw[1], LATE, M)
+        for m in (0, 1):
             times_u(0, m, False)
-        for h in range(2):
-            mix(False, u_mix[1], u_raw[1], h * H, (h + 1) * H)
-            quantise(u_codes[1], u_scale[1], u_mix[1], h * H, (h + 1) * H)
-            for m in (2 * h, 2 * h + 1):
-                times_u(1, m, True)
-                nc.scalar.activation(result[m][:], sums[m][:], GELU, bias=b_cols[:, m : m + 1])
-                nc.sync.dma_start(out[P * m : P * (m + 1), :], result[m][:])
+            times_u(1, m, True)
+            finish(m, 1)
+        quantise(u_codes[0], u_scale[0], u_mix[0], H, M)
+        quantise(u_codes[1], u_scale[1], u_mix[1], H, LATE)
+        quantise(u_codes[1], u_scale[1], u_mix[1], LATE, M)
+        for m in (2, 3):
+            times_u(0, m, False)
+            times_u(1, m, True)
+            finish(m, m - 1)

from contextlib import ExitStack

import concourse.mybir as mybir
from concourse.masks import make_identity

K, L, M, T, S = 1536, 1024, 512, 1024, 512
FLOPS = 2 * M * S * (K + L)

F32 = mybir.dt.float32
BF16 = mybir.dt.bfloat16
I32 = mybir.dt.int32
U32 = mybir.dt.uint32
U16 = mybir.dt.uint16
U8 = mybir.dt.uint8
FP8X4 = mybir.dt.float8_e4m3fn_x4
FP4X4 = mybir.dt.float4_e2m1fn_x4
MULT = mybir.AluOpType.mult
GELU = mybir.ActivationFunctionType.Gelu_apprx_tanh

P = 128
KP = 512
NX, NC = K // KP, L // KP
NM = M // P
H = S // 2
LATE = M - P


def tile_list_hmix_gelu_kernel(tc, xT, w4_words, w4_scales, c, u, wgt, b, offs, out):
    nc = tc.nc
    with ExitStack() as ctx:
        keep = ctx.enter_context(tc.tile_pool(name="keep", bufs=1))
        psum = ctx.enter_context(tc.psum_pool(name="psum", bufs=1))

        def held(shape, dtype, name):
            return keep.tile(shape, dtype, name=name, tag=name, align_bytes=64)

        offsets = keep.tile([P, S // 16], U16, name="offsets")
        weight = held([P, S], F32, "weight")
        planes = [[held([P, T], F32, "plane%d_%d" % (a, i)) for i in range(4)] for a in range(NX)]
        picked = [held([P, 4, S], F32, "picked%d" % a) for a in range(NX)]
        c_raw = [held([P, 4, S], F32, "c_raw%d" % a) for a in range(NC)]
        u_raw = [held([P, 4, M], F32, "u_raw%d" % a) for a in range(NC)]
        x_mix = [held([P, S, 4], BF16, "x_mix%d" % a) for a in range(NX)]
        c_mix = [held([P, S, 4], BF16, "c_mix%d" % a) for a in range(NC)]
        u_mix = [held([P, M, 4], BF16, "u_mix%d" % a) for a in range(NC)]
        x_codes = [None] * NX
        c_codes = [None] * NC
        u_codes = [held([P, M], U32, "u_codes%d" % a) for a in range(NC)]
        x_scale = [held([P, S], U8, "x_scale%d" % a) for a in range(NX)]
        c_scale = [held([P, S], U8, "c_scale%d" % a) for a in range(NC)]
        u_scale = [held([P, M], U8, "u_scale%d" % a) for a in range(NC)]
        w_words = held([P, NX, 2 * M], U8, "w_words")
        w_scale = held([P, NX, M], U8, "w_scale")
        b_rows = held([P, P], F32, "b_rows")
        b_cols = held([P, NM], F32, "b_cols")
        ident = held([P, P], F32, "ident")
        warm = held([P, 1], F32, "warm")
        result = [held([P, S], F32, "result%d" % m) for m in range(NM)]
        sums = [psum.tile([P, S], F32, name="sums%d" % m, tag="sums%d" % m) for m in range(NM)]
        b_turned = psum.tile([P, P], F32, name="b_turned")

        def instead(tag, shape, dtype, name):
            return keep.tile(shape, dtype, name=name, tag=tag, align_bytes=64)

        def load_plane(a, i):
            rows = xT[KP * a : KP * (a + 1), :].rearrange("(p i) t -> p i t", i=4)
            nc.sync.dma_start(planes[a][i][:], rows[:, i, :])

        def load_w_scale(q):
            nc.sync.dma_start(
                w_scale[32 * q : 32 * q + 4, :, :].bitcast(I32),
                w4_scales[:, 4 * q : 4 * q + 4, :].rearrange("a r n -> r a n").bitcast(I32),
            )

        def load_raw(tiles, src, a, lo, hi):
            rows = src[KP * a : KP * (a + 1), :].rearrange("(p i) w -> p i w", i=4)
            nc.sync.dma_start(tiles[a][:, :, lo:hi], rows[:, :, lo:hi])

        def gather(a, i):
            for h in range(2):
                cols = slice(h * H, (h + 1) * H)
                nc.vector.tensor_tensor(
                    picked[a][:, i, cols],
                    planes[a][i][:].indirect(offsets[:, h * H // 16 : (h + 1) * H // 16]),
                    weight[:, cols],
                    MULT,
                )

        def mix(on_scalar, mixed, raw, lo, hi):
            src = raw[:, :, lo:hi].rearrange("p i (g w) -> p g i w", w=4)
            dst = mixed[:, lo:hi, :].rearrange("p (g w) i -> p g i w", w=4)
            if on_scalar:
                nc.scalar.copy(dst, src)
            else:
                nc.vector.tensor_copy(dst, src)

        def quantise(codes, scale, mixed, lo, hi):
            nc.vector.quantize_mx(
                out=codes[:, lo:hi].bitcast(FP8X4),
                scales=scale[:, lo:hi],
                in_=mixed[:, lo:hi, :].rearrange("p w i -> p (w i)"),
            )

        def times_w4(a, start):
            for m in range(NM):
                nc.tensor.matmul_mx(
                    out=sums[m][:],
                    lhsT=w_words[:, a, 2 * P * m : 2 * P * (m + 1)].bitcast(FP4X4),
                    lhsT_scale=w_scale[:, a, P * m : P * (m + 1)],
                    rhs=x_codes[a][:].bitcast(FP8X4),
                    rhs_scale=x_scale[a][:],
                    start=start,
                    stop=False,
                )

        def times_u(a, m, stop):
            cols = slice(P * m, P * (m + 1))
            nc.tensor.matmul_mx(
                out=sums[m][:],
                lhsT=u_codes[a][:, cols].bitcast(FP8X4),
                lhsT_scale=u_scale[a][:, cols],
                rhs=c_codes[a][:].bitcast(FP8X4),
                rhs_scale=c_scale[a][:],
                start=False,
                stop=stop,
            )

        def finish(m, pieces):
            width = S // pieces
            for j in range(pieces):
                cols = slice(width * j, width * (j + 1))
                nc.scalar.activation(result[m][:, cols], sums[m][:, cols], GELU, bias=b_cols[:, m : m + 1])
                nc.sync.dma_start(out[P * m : P * (m + 1), cols], result[m][:, cols])

        nc.gpsimd.memset(w_scale[:].rearrange("p a n -> p (a n)").bitcast(I32), 0)
        nc.gpsimd.memset(b_rows[:], 0.0)
        nc.gpsimd.memset(warm[:], 0.0)
        make_identity(nc, ident[:])
        nc.scalar.activation(warm[:], warm[:], GELU)

        nc.sync.dma_start(offsets[:], offs)
        nc.sync.dma_start(weight[:, 0:H], wgt[:, 0:H])
        load_plane(0, 0)
        nc.sync.dma_start(weight[:, H:S], wgt[:, H:S])
        for i in range(1, 4):
            load_plane(0, i)
        for i in range(3):
            load_plane(1, i)
            load_w_scale(i)
        load_raw(c_raw, c, 0, 0, S)
        load_w_scale(3)
        load_plane(1, 3)
        nc.sync.dma_start(b_rows[0:NM, :], b.rearrange("(m p) -> m p", p=P))
        for i in range(3):
            load_plane(2, i)
        load_raw(c_raw, c, 1, 0, S)
        load_plane(2, 3)
        nc.sync.dma_start(w_words[:], w4_words.rearrange("a p n -> p a n"))
        load_raw(u_raw, u, 0, 0, M)
        load_raw(u_raw, u, 1, 0, H)
        load_raw(u_raw, u, 1, H, M)

        for i in range(4):
            gather(0, i)
        mix(True, x_mix[0], picked[0], 0, S)
        for i in range(3):
            gather(1, i)
        mix(True, c_mix[0], c_raw[0], 0, S)
        x_codes[0] = instead("plane1_2", [P, S], U32, "x_codes0")
        quantise(x_codes[0], x_scale[0], x_mix[0], 0, S)
        gather(1, 3)
        mix(True, x_mix[1], picked[1], 0, S)
        for i in range(3):
            gather(2, i)
        x_codes[1] = instead("plane2_2", [P, S], U32, "x_codes1")
        quantise(x_codes[1], x_scale[1], x_mix[1], 0, S)
        mix(True, c_mix[1], c_raw[1], 0, S)
        nc.tensor.transpose(b_turned[:], b_rows[:], ident[:])
        nc.scalar.copy(b_cols[:], b_turned[:, 0:NM])
        gather(2, 3)
        mix(False, x_mix[2], picked[2], 0, H)
        mix(True, x_mix[2], picked[2], H, S)
        c_codes[0] = instead("plane2_3", [P, S], U32, "c_codes0")
        c_codes[1] = held([P, S], U32, "c_codes1")
        quantise(c_codes[0], c_scale[0], c_mix[0], 0, S)
        quantise(c_codes[1], c_scale[1], c_mix[1], 0, S)
        times_w4(0, True)
        times_w4(1, False)
        x_codes[2] = held([P, S], U32, "x_codes2")
        quantise(x_codes[2], x_scale[2], x_mix[2], 0, S)
        times_w4(2, False)
        mix(True, u_mix[0], u_raw[0], 0, H)
        mix(True, u_mix[0], u_raw[0], H, M)
        mix(False, u_mix[1], u_raw[1], 0, H)
        quantise(u_codes[0], u_scale[0], u_mix[0], 0, H)
        quantise(u_codes[1], u_scale[1], u_mix[1], 0, H)
        mix(True, u_mix[1], u_raw[1], H, LATE)
        mix(False, u_mix[1], u_raw[1], LATE, M)
        for m in (0, 1):
            times_u(0, m, False)
            times_u(1, m, True)
            finish(m, 1)
        quantise(u_codes[0], u_scale[0], u_mix[0], H, M)
        quantise(u_codes[1], u_scale[1], u_mix[1], H, LATE)
        quantise(u_codes[1], u_scale[1], u_mix[1], LATE, M)
        for m in (2, 3):
            times_u(0, m, False)
            times_u(1, m, True)
            finish(m, m - 1)
